import numpy as np
import ml_dtypes


def mxq(x, axis, fmt="e4m3"):
    dtype, down = {"e4m3": (ml_dtypes.float8_e4m3fn, 7), "e5m2": (ml_dtypes.float8_e5m2, 14)}[fmt]
    v = np.moveaxis(np.asarray(x, np.float32).astype(ml_dtypes.bfloat16).astype(np.float64), axis, -1)
    blocks = v.reshape(v.shape[:-1] + (-1, 32))
    amax = np.abs(blocks).max(-1, keepdims=True)
    byte = np.maximum(np.where(amax > 0, np.frexp(amax)[1] - 1 + 127, 0) - down, 1)
    scale = np.exp2(byte - 127.0)
    codes = (blocks / scale).astype(np.float32).astype(dtype).astype(np.float64)
    return np.moveaxis((codes * scale).reshape(v.shape), -1, axis)


WIDE = False


def mx_kscale(k):
    if not WIDE:
        return np.ones(k)
    levels = np.array([30, -30])
    if k % 512:
        return np.exp2(np.random.permutation(np.resize(levels, k // 32))).repeat(32)
    a = np.empty((k // 512, 16))
    for p in range(k // 512):
        a[p, :8] = np.random.permutation(np.resize(levels, 8))
        for g in range(8):
            far = levels[np.abs(levels - a[p, g]) >= 10]
            a[p, g + 8] = far[np.random.randint(len(far))]
    return np.exp2(a.ravel()).repeat(32)


def f64(x):
    return np.asarray(x).astype(np.float64)


def striped(idx):
    return np.tile(np.asarray(idx).reshape(-1, 16).T, (8, 1)).astype(np.uint16)


def unstriped(offs):
    return offs[:16].T.reshape(-1).astype(np.int64)


E2M1 = np.array([0.0, 0.5, 1.0, 1.5, 2.0, 3.0, 4.0, 6.0, -0.0, -0.5, -1.0, -1.5, -2.0, -3.0, -4.0, -6.0])


def pack_weight(w, fmt):
    k, n = w.shape
    w = f64(np.asarray(w, np.float32).astype(ml_dtypes.bfloat16)).reshape(k // 32, 32, n)
    amax = np.abs(w).max(1)
    if fmt in ("e4m3", "e5m2"):
        byte = np.frexp(amax)[1] - 1 + 127 - (7 if fmt == "e4m3" else 14)
    else:
        mant, ex = np.frexp(amax / 6.0)
        byte = np.where(mant > 0.5, ex, ex - 1) + 127
    byte = np.clip(np.where(amax > 0, byte, 1), 1, 254)
    scaled = (w * np.exp2(127.0 - byte)[:, None, :]).reshape(k, n).astype(np.float32)
    by_word = np.ascontiguousarray(scaled.reshape(k // 512, 128, 4, n).transpose(0, 1, 3, 2))
    if fmt in ("e4m3", "e5m2"):
        words = by_word.astype(ml_dtypes.float8_e4m3fn if fmt == "e4m3" else ml_dtypes.float8_e5m2).view(np.uint8)
    else:
        c = by_word.astype(ml_dtypes.float4_e2m1fn).view(np.uint8) & 0xF
        words = (c[..., 0::2] | (c[..., 1::2] << 4)).reshape(k // 512, 128, 2 * n)
    return np.ascontiguousarray(words), np.ascontiguousarray(byte.astype(np.uint8).reshape(k // 512, 16, n))


def unpack_weight(words, scales, fmt):
    g, _, n = scales.shape
    words = np.ascontiguousarray(words).reshape(g, 128, n, -1)
    if fmt in ("e4m3", "e5m2"):
        vals = words.view(ml_dtypes.float8_e4m3fn if fmt == "e4m3" else ml_dtypes.float8_e5m2).astype(np.float64)
    else:
        nib = np.empty((g, 128, n, 4), np.uint8)
        nib[..., 0::2] = words & 0xF
        nib[..., 1::2] = words >> 4
        vals = E2M1[nib]
    vals = vals * np.repeat(np.exp2(scales.astype(np.float64) - 127.0), 8, axis=1)[..., None]
    return vals.transpose(0, 1, 3, 2).reshape(g * 512, n)


K, T, J, R, C, O, N, L, E = 512, 2048, 256, 512, 512, 256, 256, 512, 1024


def setup_inputs():
    n = np.random.standard_normal
    idx = np.random.permutation(T)[:J]
    idx2 = np.random.permutation(T)[:J]
    idx3 = np.random.permutation(C)[:J]
    idx4 = np.random.permutation(C)[:J]
    idx5 = np.random.permutation(C)[:O]
    idx6 = np.random.permutation(C)[:O]
    idx7 = np.random.permutation(E)[:O]
    fk = mx_kscale(K)
    fr = mx_kscale(R)
    fl = mx_kscale(L)
    xtp = pack_weight(n((K, T)) / fk[:, None], "e2m1")
    wp = pack_weight(n((K, R)) * 1 / np.sqrt(K) * fk[:, None] * fr, "e4m3")
    w2p = pack_weight(n((K, R)) * 1 / np.sqrt(K) * fk[:, None] * fr, "e5m2")
    wbp = pack_weight(n((R, N)) * 1 / np.sqrt(R) / fr[:, None], "e2m1")
    sxp = pack_weight(n((L, O)) / fl[:, None], "e4m3")
    wsp = pack_weight(n((L, N)) * 1 / np.sqrt(L) * fl[:, None], "e4m3")
    return {
        "xt_words": xtp[0],
        "xt_scales": xtp[1],
        "w_words": wp[0],
        "w_scales": wp[1],
        "w2_words": w2p[0],
        "w2_scales": w2p[1],
        "wb_words": wbp[0],
        "wb_scales": wbp[1],
        "sx_words": sxp[0],
        "sx_scales": sxp[1],
        "ws_words": wsp[0],
        "ws_scales": wsp[1],
        "tz": (n((N, E))).astype(np.float32),
        "offs": striped(idx),
        "offs2": striped(idx2),
        "offs3": striped(idx3),
        "offs4": striped(idx4),
        "offs5": striped(idx5),
        "offs6": striped(idx6),
        "offs7": striped(idx7),
    }


def reference(xt_words, xt_scales, w_words, w_scales, w2_words, w2_scales, wb_words, wb_scales, sx_words, sx_scales, ws_words, ws_scales, tz, offs, offs2, offs3, offs4, offs5, offs6, offs7):
    idx = unstriped(offs)
    idx2 = unstriped(offs2)
    idx3 = unstriped(offs3)
    idx4 = unstriped(offs4)
    idx5 = unstriped(offs5)
    idx6 = unstriped(offs6)
    idx7 = unstriped(offs7)
    xtu = unpack_weight(xt_words, xt_scales, "e2m1")
    wu = unpack_weight(w_words, w_scales, "e4m3")
    w2u = unpack_weight(w2_words, w2_scales, "e5m2")
    wbu = unpack_weight(wb_words, wb_scales, "e2m1")
    sxu = unpack_weight(sx_words, sx_scales, "e4m3")
    wsu = unpack_weight(ws_words, ws_scales, "e4m3")
    xtidxg = xtu[:, idx]
    a = wu.T @ xtidxg
    xtidx2g = xtu[:, idx2]
    b = w2u.T @ xtidx2g
    pw = np.zeros((R, C))
    pw[:, idx3] = a
    pv = np.zeros((R, C))
    pv[:, idx4] = b
    hid = np.maximum(pw[:, idx5], pv[:, idx6])
    hidq = mxq(hid, 0, "e5m2")
    p = wbu.T @ hidq + wsu.T @ sxu
    y = p + f64(tz)[:, idx7]
    return y

@@ -1,0 +1,202 @@
+from contextlib import ExitStack
+
+import concourse.mybir as mybir
+
+K, T, J, R, C, O, N, L, E = 512, 2048, 256, 512, 512, 256, 256, 512, 1024
+FLOPS = 2 * (2 * K * R * J + R * N * O + L * N * O)
+
+F32 = mybir.dt.float32
+BF16 = mybir.dt.bfloat16
+I32 = mybir.dt.int32
+U32 = mybir.dt.uint32
+U16 = mybir.dt.uint16
+U8 = mybir.dt.uint8
+E4M3 = mybir.dt.float8_e4m3fn_x4
+E5M2 = mybir.dt.float8_e5m2_x4
+E2M1 = mybir.dt.float4_e2m1fn_x4
+COPY = mybir.ActivationFunctionType.Copy
+ALU = mybir.AluOpType
+
+P = 128
+PACK = 4
+
+
+def tile_list_ahead_twoboards_skip_tabled_kernel(
+    tc, xt_words, xt_scales, w_words, w_scales, w2_words, w2_scales, wb_words, wb_scales,
+    sx_words, sx_scales, ws_words, ws_scales, tz, offs, offs2, offs3, offs4, offs5, offs6, offs7, out,
+):
+    nc = tc.nc
+
+    def load_list(pool, source, name):
+        tile = pool.tile([P, J // 16], U16, name=name)
+        nc.sync.dma_start(tile[:], source)
+        return tile
+
+    def load_words(tile, words):
+        nc.sync.dma_start(tile[:].bitcast(I32), words.bitcast(I32))
+
+    def load_scales(tile, scales):
+        for q in range(4):
+            nc.sync.dma_start(
+                tile[32 * q : 32 * q + 4, :].bitcast(I32), scales[0, 4 * q : 4 * q + 4, :].bitcast(I32)
+            )
+
+    def load_scales_repeated(tile, scales):
+        for q in range(4):
+            rows = scales[0, 4 * q : 4 * q + 4, :].bitcast(I32)
+            nc.sync.dma_start(
+                tile[32 * q : 32 * q + 32, :].bitcast(I32),
+                rows.unsqueeze(0).to_broadcast([8, 4, rows.shape[1]]),
+            )
+
+    def move(engine, dst, src):
+        if engine == "vector":
+            nc.vector.tensor_copy(dst, src)
+        else:
+            nc.scalar.activation(dst, src, COPY)
+
+    with ExitStack() as ctx:
+        lists = ctx.enter_context(tc.tile_pool(name="lists", bufs=1))
+        keep = ctx.enter_context(tc.tile_pool(name="keep", bufs=1))
+        psum = ctx.enter_context(tc.psum_pool(name="psum", bufs=1))
+
+        xt_w = keep.tile([P, T], U16, align_bytes=64)
+        xt_s = keep.tile([P, T], U8, align_bytes=64)
+        w_raw = keep.tile([P, R], U32, align_bytes=64)
+        w_raw_s = keep.tile([P, R], U8, align_bytes=64)
+        w2_raw = keep.tile([P, R], U32, align_bytes=64)
+        w2_raw_s = keep.tile([P, R], U8, align_bytes=64)
+        wb_w = keep.tile([P, N], U16, align_bytes=64)
+        wb_s = keep.tile([P, N], U8, align_bytes=64)
+        ws_w = keep.tile([P, N], U32, align_bytes=64)
+        ws_s = keep.tile([P, N], U8, align_bytes=64)
+        sx_w = keep.tile([P, O], U32, align_bytes=64)
+        sx_s = keep.tile([P, O], U8, align_bytes=64)
+        tz_rows = [keep.tile([P, E], F32, name=f"tz{h}") for h in range(2)]
+        boards = [[keep.tile([P, C], F32, name=f"board{b}{t}") for t in range(PACK)] for b in range(2)]
+
+        nc.vector.memset(xt_s[:].bitcast(I32), 0)
+        for t in range(PACK):
+            nc.gpsimd.memset(boards[0][t][:].bitcast(I32), 0)
+
+        load_scales_repeated(w_raw_s, w_scales)
+        load_words(xt_w, xt_words[0])
+        l1 = load_list(lists, offs, "l1")
+        load_words(w_raw, w_words[0].rearrange("p n t -> p (n t)"))
+        load_scales(xt_s, xt_scales)
+        load_words(w2_raw, w2_words[0].rearrange("p n t -> p (n t)"))
+        l2 = load_list(lists, offs2, "l2")
+        l3 = load_list(lists, offs3, "l3")
+        load_scales_repeated(w2_raw_s, w2_scales)
+        l4 = load_list(lists, offs4, "l4")
+        l5 = load_list(lists, offs5, "l5")
+        l6 = load_list(lists, offs6, "l6")
+        l7 = load_list(lists, offs7, "l7")
+        load_words(ws_w, ws_words[0].rearrange("p n t -> p (n t)"))
+        load_words(sx_w, sx_words[0].rearrange("p n t -> p (n t)"))
+        load_words(wb_w, wb_words[0])
+        load_scales(ws_s, ws_scales)
+        load_scales(sx_s, sx_scales)
+        load_scales(wb_s, wb_scales)
+        for h in range(2):
+            nc.sync.dma_start(tz_rows[h][:], tz[P * h : P * (h + 1), :])
+
+        def first_stage(b, tokens, raw, raw_s, fmt, banks):
+            xg_w = keep.tile([P, J], U16, align_bytes=64, name=f"xg_w{b}")
+            xg_s = keep.tile([P, J], U8, align_bytes=64, name=f"xg_s{b}")
+            dealt = keep.tile([P, R], U32, align_bytes=64, name=f"dealt{b}")
+            dealt_s = keep.tile([P, R], U8, align_bytes=64, name=f"dealt_s{b}")
+            nc.vector.tensor_copy(xg_w[:], xt_w[:].indirect(tokens[:]))
+            nc.vector.tensor_copy(xg_s[:], xt_s[:].indirect(tokens[:]))
+            nc.scalar.copy(
+                dealt[:].rearrange("p (t c i) -> p c t i", t=PACK, i=4),
+                raw[:].rearrange("p (c i t) -> p c t i", t=PACK, i=4),
+            )
+            nc.vector.tensor_copy(
+                dealt_s[:].rearrange("p (t m) -> p t m", t=PACK),
+                raw_s[:].rearrange("p (m t) -> p t m", t=PACK),
+            )
+            for t in range(PACK):
+                cols = slice(P * t, P * (t + 1))
+                nc.tensor.matmul_mx(
+                    out=banks[t], lhsT=dealt[:, cols].bitcast(fmt), lhsT_scale=dealt_s[:, cols],
+                    rhs=xg_w[:].bitcast(E2M1), rhs_scale=xg_s[:], start=True, stop=True,
+                )
+
+        a_banks = [psum.tile([P, J], F32, name=f"a{t}") for t in range(PACK)]
+        b_banks = [psum.tile([P, 2, J], F32, name=f"b{u}") for u in range(2)]
+        first_stage(0, l1, w_raw, w_raw_s, E4M3, [a_banks[t][:] for t in range(PACK)])
+        first_stage(1, l2, w2_raw, w2_raw_s, E5M2, [b_banks[t // 2][:, t % 2, :] for t in range(PACK)])
+
+        for t in range(PACK):
+            nc.gpsimd.memset(boards[1][t][:].bitcast(I32), 0)
+
+        p_banks = [psum.tile([P, 2, P], F32, name=f"p{u}") for u in range(2)]
+        for u in range(2):
+            reads = slice(P * u, P * (u + 1))
+            for h in range(2):
+                cols = slice(P * h, P * (h + 1))
+                nc.tensor.matmul_mx(
+                    out=p_banks[u][:, h, :], lhsT=ws_w[:, cols].bitcast(E4M3), lhsT_scale=ws_s[:, cols],
+                    rhs=sx_w[:, reads].bitcast(E4M3), rhs_scale=sx_s[:, reads], start=(h == 0), stop=False,
+                )
+
+        a_sb = [keep.tile([P, J], F32, name=f"a_sb{t}") for t in range(PACK)]
+        b_sb = [keep.tile([P, 2, J], F32, name=f"b_sb{u}") for u in range(2)]
+        picked = [keep.tile([P, PACK, O], F32, name=f"picked{b}") for b in range(2)]
+        put, get = (l3, l4), (l5, l6)
+
+        def scatter(engine, b, t):
+            src = a_sb[t][:] if b == 0 else b_sb[t // 2][:, t % 2, :]
+            move(engine, boards[b][t][:].indirect(put[b][:]), src)
+
+        def gather(engine, b, t):
+            move(engine, picked[b][:, t, :], boards[b][t][:].indirect(get[b][:]))
+
+        for t in (1, 0, 3, 2):
+            nc.scalar.copy(a_sb[t][:], a_banks[t][:])
+        scatter("vector", 0, 1)
+        scatter("scalar", 0, 0)
+        scatter("vector", 0, 3)
+        for u in range(2):
+            nc.scalar.copy(b_sb[u][:], b_banks[u][:])
+        scatter("scalar", 0, 2)
+        scatter("vector", 1, 1)
+        scatter("scalar", 1, 0)
+        scatter("vector", 1, 3)
+        scatter("scalar", 1, 2)
+        for b, t in ((0, 0), (0, 1), (0, 2), (0, 3), (1, 1)):
+            gather("vector", b, t)
+        for b, t in ((1, 0), (1, 2), (1, 3)):
+            gather("scalar", b, t)
+
+        entries = keep.tile([P, 2, O], F32)
+        for h in range(2):
+            nc.scalar.activation(entries[:, h, :], tz_rows[h][:].indirect(l7[:]), COPY)
+
+        hid = [keep.tile([P, P, PACK], BF16, align_bytes=64, name=f"hid{u}") for u in range(2)]
+        for u in range(2):
+            reads = slice(P * u, P * (u + 1))
+            nc.vector.tensor_tensor(
+                hid[u][:].rearrange("p (c i) t -> p c t i", i=4),
+                picked[0][:, :, reads].rearrange("p t (c i) -> p c t i", i=4),
+                picked[1][:, :, reads].rearrange("p t (c i) -> p c t i", i=4),
+                ALU.max,
+            )
+        hid_w = [keep.tile([P, P], U32, align_bytes=64, name=f"hid_w{u}") for u in range(2)]
+        hid_s = [keep.tile([P, P], U8, align_bytes=64, name=f"hid_s{u}") for u in range(2)]
+        for u in range(2):
+            nc.vector.quantize_mx(
+                out=hid_w[u][:].bitcast(E5M2), scales=hid_s[u][:], in_=hid[u][:].rearrange("p o t -> p (o t)")
+            )
+            for h in range(2):
+                cols = slice(P * h, P * (h + 1))
+                nc.tensor.matmul_mx(
+                    out=p_banks[u][:, h, :], lhsT=wb_w[:, cols].bitcast(E2M1), lhsT_scale=wb_s[:, cols],
+                    rhs=hid_w[u][:].bitcast(E5M2), rhs_scale=hid_s[u][:], start=False, stop=(h == 1),
+                )
+        for u in range(2):
+            reads = slice(P * u, P * (u + 1))
+            result = keep.tile([P, 2, P], F32, name=f"result{u}")
+            nc.vector.tensor_tensor(result[:], p_banks[u][:], entries[:, :, reads], ALU.add)
+            nc.sync.dma_start(out[:, reads].rearrange("(h p) o -> p h o", h=2), result[:])

@@ -65,7 +65,7 @@ def tile_list_ahead_twoboards_skip_tabled_kernel(
         w_raw = keep.tile([P, R], U32, align_bytes=64)
         w_raw_s = keep.tile([P, R], U8, align_bytes=64)
         w2_raw = keep.tile([P, R], U32, align_bytes=64)
-        w2_raw_s = keep.tile([P, R], U8, align_bytes=64)
+        w2_raw_s = keep.tile([P, R], U8, align_bytes=64, tag="reused")
         wb_w = keep.tile([P, N], U16, align_bytes=64)
         wb_s = keep.tile([P, N], U8, align_bytes=64)
         ws_w = keep.tile([P, N], U32, align_bytes=64)
@@ -76,21 +76,24 @@ def tile_list_ahead_twoboards_skip_tabled_kernel(
         boards = [[keep.tile([P, C], F32, name=f"board{b}{t}") for t in range(PACK)] for b in range(2)]
 
         nc.vector.memset(xt_s[:].bitcast(I32), 0)
-        for t in range(PACK):
-            nc.gpsimd.memset(boards[0][t][:].bitcast(I32), 0)
+        for b in range(2):
+            for t in range(PACK):
+                nc.vector.memset(boards[b][t][:].bitcast(I32), 0)
 
         load_scales_repeated(w_raw_s, w_scales)
         load_words(xt_w, xt_words[0])
         l1 = load_list(lists, offs, "l1")
+        l2 = load_list(lists, offs2, "l2")
         load_words(w_raw, w_words[0].rearrange("p n t -> p (n t)"))
         load_scales(xt_s, xt_scales)
         load_words(w2_raw, w2_words[0].rearrange("p n t -> p (n t)"))
-        l2 = load_list(lists, offs2, "l2")
         l3 = load_list(lists, offs3, "l3")
         load_scales_repeated(w2_raw_s, w2_scales)
         l4 = load_list(lists, offs4, "l4")
         l5 = load_list(lists, offs5, "l5")
         l6 = load_list(lists, offs6, "l6")
+        for h in range(2):
+            nc.sync.dma_start(tz_rows[h][:], tz[P * h : P * (h + 1), :])
         l7 = load_list(lists, offs7, "l7")
         load_words(ws_w, ws_words[0].rearrange("p n t -> p (n t)"))
         load_words(sx_w, sx_words[0].rearrange("p n t -> p (n t)"))
@@ -98,40 +101,79 @@ def tile_list_ahead_twoboards_skip_tabled_kernel(
         load_scales(ws_s, ws_scales)
         load_scales(sx_s, sx_scales)
         load_scales(wb_s, wb_scales)
-        for h in range(2):
-            nc.sync.dma_start(tz_rows[h][:], tz[P * h : P * (h + 1), :])
 
-        def first_stage(b, tokens, raw, raw_s, fmt, banks):
-            xg_w = keep.tile([P, J], U16, align_bytes=64, name=f"xg_w{b}")
-            xg_s = keep.tile([P, J], U8, align_bytes=64, name=f"xg_s{b}")
-            dealt = keep.tile([P, R], U32, align_bytes=64, name=f"dealt{b}")
-            dealt_s = keep.tile([P, R], U8, align_bytes=64, name=f"dealt_s{b}")
-            nc.vector.tensor_copy(xg_w[:], xt_w[:].indirect(tokens[:]))
-            nc.vector.tensor_copy(xg_s[:], xt_s[:].indirect(tokens[:]))
+        xg_w = [keep.tile([P, J], U16, align_bytes=64, name=f"xg_w{b}") for b in range(2)]
+        xg_s = [keep.tile([P, J], U8, align_bytes=64, name=f"xg_s{b}") for b in range(2)]
+        dealt = [keep.tile([P, R], U32, align_bytes=64, name=f"dealt{b}") for b in range(2)]
+        dealt_s = [keep.tile([P, R], U8, align_bytes=64, name=f"dealt_s{b}") for b in range(2)]
+
+        def deal_words(b, raw):
             nc.scalar.copy(
-                dealt[:].rearrange("p (t c i) -> p c t i", t=PACK, i=4),
+                dealt[b][:].rearrange("p (t c i) -> p c t i", t=PACK, i=4),
                 raw[:].rearrange("p (c i t) -> p c t i", t=PACK, i=4),
             )
+
+        def deal_scales(b, raw_s):
             nc.vector.tensor_copy(
-                dealt_s[:].rearrange("p (t m) -> p t m", t=PACK),
+                dealt_s[b][:].rearrange("p (t m) -> p t m", t=PACK),
                 raw_s[:].rearrange("p (m t) -> p t m", t=PACK),
             )
+
+        def first_stage(b, fmt, banks):
             for t in range(PACK):
                 cols = slice(P * t, P * (t + 1))
                 nc.tensor.matmul_mx(
-                    out=banks[t], lhsT=dealt[:, cols].bitcast(fmt), lhsT_scale=dealt_s[:, cols],
-                    rhs=xg_w[:].bitcast(E2M1), rhs_scale=xg_s[:], start=True, stop=True,
+                    out=banks[t], lhsT=dealt[b][:, cols].bitcast(fmt), lhsT_scale=dealt_s[b][:, cols],
+                    rhs=xg_w[b][:].bitcast(E2M1), rhs_scale=xg_s[b][:], start=True, stop=True,
                 )
 
+        deal_scales(0, w_raw_s)
+        deal_words(0, w_raw)
+        deal_words(1, w2_raw)
+        for b, tokens in enumerate((l1, l2)):
+            nc.vector.tensor_copy(xg_w[b][:], xt_w[:].indirect(tokens[:]))
+        for b, tokens in enumerate((l1, l2)):
+            nc.vector.tensor_copy(xg_s[b][:], xt_s[:].indirect(tokens[:]))
         a_banks = [psum.tile([P, J], F32, name=f"a{t}") for t in range(PACK)]
-        b_banks = [psum.tile([P, 2, J], F32, name=f"b{u}") for u in range(2)]
-        first_stage(0, l1, w_raw, w_raw_s, E4M3, [a_banks[t][:] for t in range(PACK)])
-        first_stage(1, l2, w2_raw, w2_raw_s, E5M2, [b_banks[t // 2][:, t % 2, :] for t in range(PACK)])
+        b_banks = [psum.tile([P, 2, J], F32, name=f"b{u}", tag=f"late{u}") for u in range(2)]
+        first_stage(0, E4M3, [a_banks[t][:] for t in range(PACK)])
+        deal_scales(1, w2_raw_s)
+        first_stage(1, E5M2, [b_banks[t % 2][:, t // 2, :] for t in range(PACK)])
+
+        a_sb = [keep.tile([P, J], F32, name=f"a_sb{t}") for t in range(PACK - 1)]
+        a_sb.append(keep.tile([P, J], F32, align_bytes=64, name="a_sb3", tag="reused"))
+        b_sb = [keep.tile([P, 2, J], F32, name=f"b_sb{u}") for u in range(2)]
+        picked = [keep.tile([P, PACK, O], F32, name=f"picked{b}") for b in range(2)]
+        put, get = (l3, l4), (l5, l6)
+
+        def scatter(engine, b, t):
+            src = a_sb[t][:] if b == 0 else b_sb[t % 2][:, t // 2, :]
+            move(engine, boards[b][t][:].indirect(put[b][:]), src)
+
+        def gather(engine, b, t):
+            move(engine, picked[b][:, t, :], boards[b][t][:].indirect(get[b][:]))
+
+        owner = ("scalar", "vector")
+
+        def leave_psum(engine, dst, src):
+            if engine == "vector":
+                nc.vector.tensor_copy(dst, src)
+            else:
+                nc.scalar.copy(dst, src)
 
         for t in range(PACK):
-            nc.gpsimd.memset(boards[1][t][:].bitcast(I32), 0)
+            leave_psum(owner[t % 2], a_sb[t][:], a_banks[t][:])
+        for t in range(PACK):
+            scatter(owner[t % 2], 0, t)
+        for u in (1, 0):
+            nc.scalar.copy(b_sb[u][:], b_banks[u][:])
+        for t in range(PACK):
+            scatter(owner[t % 2], 1, t)
+        for t in range(PACK):
+            for b in range(2):
+                gather(owner[t % 2], b, t)
 
-        p_banks = [psum.tile([P, 2, P], F32, name=f"p{u}") for u in range(2)]
+        p_banks = [psum.tile([P, 2, P], F32, name=f"p{u}", tag=f"late{u}") for u in range(2)]
         for u in range(2):
             reads = slice(P * u, P * (u + 1))
             for h in range(2):
@@ -141,36 +183,7 @@ def tile_list_ahead_twoboards_skip_tabled_kernel(
                     rhs=sx_w[:, reads].bitcast(E4M3), rhs_scale=sx_s[:, reads], start=(h == 0), stop=False,
                 )
 
-        a_sb = [keep.tile([P, J], F32, name=f"a_sb{t}") for t in range(PACK)]
-        b_sb = [keep.tile([P, 2, J], F32, name=f"b_sb{u}") for u in range(2)]
-        picked = [keep.tile([P, PACK, O], F32, name=f"picked{b}") for b in range(2)]
-        put, get = (l3, l4), (l5, l6)
-
-        def scatter(engine, b, t):
-            src = a_sb[t][:] if b == 0 else b_sb[t // 2][:, t % 2, :]
-            move(engine, boards[b][t][:].indirect(put[b][:]), src)
-
-        def gather(engine, b, t):
-            move(engine, picked[b][:, t, :], boards[b][t][:].indirect(get[b][:]))
-
-        for t in (1, 0, 3, 2):
-            nc.scalar.copy(a_sb[t][:], a_banks[t][:])
-        scatter("vector", 0, 1)
-        scatter("scalar", 0, 0)
-        scatter("vector", 0, 3)
-        for u in range(2):
-            nc.scalar.copy(b_sb[u][:], b_banks[u][:])
-        scatter("scalar", 0, 2)
-        scatter("vector", 1, 1)
-        scatter("scalar", 1, 0)
-        scatter("vector", 1, 3)
-        scatter("scalar", 1, 2)
-        for b, t in ((0, 0), (0, 1), (0, 2), (0, 3), (1, 1)):
-            gather("vector", b, t)
-        for b, t in ((1, 0), (1, 2), (1, 3)):
-            gather("scalar", b, t)
-
-        entries = keep.tile([P, 2, O], F32)
+        entries = keep.tile([P, 2, O], F32, tag="board12")
         for h in range(2):
             nc.scalar.activation(entries[:, h, :], tz_rows[h][:].indirect(l7[:]), COPY)
 

from contextlib import ExitStack

import concourse.mybir as mybir

K, T, J, R, C, O, N, L, E = 512, 2048, 256, 512, 512, 256, 256, 512, 1024
FLOPS = 2 * (2 * K * R * J + R * N * O + L * N * O)

F32 = mybir.dt.float32
BF16 = mybir.dt.bfloat16
I32 = mybir.dt.int32
U32 = mybir.dt.uint32
U16 = mybir.dt.uint16
U8 = mybir.dt.uint8
E4M3 = mybir.dt.float8_e4m3fn_x4
E5M2 = mybir.dt.float8_e5m2_x4
E2M1 = mybir.dt.float4_e2m1fn_x4
COPY = mybir.ActivationFunctionType.Copy
ALU = mybir.AluOpType

P = 128
PACK = 4


def tile_list_ahead_twoboards_skip_tabled_kernel(
    tc, xt_words, xt_scales, w_words, w_scales, w2_words, w2_scales, wb_words, wb_scales,
    sx_words, sx_scales, ws_words, ws_scales, tz, offs, offs2, offs3, offs4, offs5, offs6, offs7, out,
):
    nc = tc.nc

    def load_list(pool, source, name):
        tile = pool.tile([P, J // 16], U16, name=name)
        nc.sync.dma_start(tile[:], source)
        return tile

    def load_words(tile, words):
        nc.sync.dma_start(tile[:].bitcast(I32), words.bitcast(I32))

    def load_scales(tile, scales):
        for q in range(4):
            nc.sync.dma_start(
                tile[32 * q : 32 * q + 4, :].bitcast(I32), scales[0, 4 * q : 4 * q + 4, :].bitcast(I32)
            )

    def load_scales_repeated(tile, scales):
        for q in range(4):
            rows = scales[0, 4 * q : 4 * q + 4, :].bitcast(I32)
            nc.sync.dma_start(
                tile[32 * q : 32 * q + 32, :].bitcast(I32),
                rows.unsqueeze(0).to_broadcast([8, 4, rows.shape[1]]),
            )

    def move(engine, dst, src):
        if engine == "vector":
            nc.vector.tensor_copy(dst, src)
        else:
            nc.scalar.activation(dst, src, COPY)

    with ExitStack() as ctx:
        lists = ctx.enter_context(tc.tile_pool(name="lists", bufs=1))
        keep = ctx.enter_context(tc.tile_pool(name="keep", bufs=1))
        psum = ctx.enter_context(tc.psum_pool(name="psum", bufs=1))

        xt_w = keep.tile([P, T], U16, align_bytes=64)
        xt_s = keep.tile([P, T], U8, align_bytes=64)
        w_raw = keep.tile([P, R], U32, align_bytes=64)
        w_raw_s = keep.tile([P, R], U8, align_bytes=64)
        w2_raw = keep.tile([P, R], U32, align_bytes=64)
        w2_raw_s = keep.tile([P, R], U8, align_bytes=64, tag="reused")
        wb_w = keep.tile([P, N], U16, align_bytes=64)
        wb_s = keep.tile([P, N], U8, align_bytes=64)
        ws_w = keep.tile([P, N], U32, align_bytes=64)
        ws_s = keep.tile([P, N], U8, align_bytes=64)
        sx_w = keep.tile([P, O], U32, align_bytes=64)
        sx_s = keep.tile([P, O], U8, align_bytes=64)
        tz_rows = [keep.tile([P, E], F32, name=f"tz{h}") for h in range(2)]
        boards = [[keep.tile([P, C], F32, name=f"board{b}{t}") for t in range(PACK)] for b in range(2)]

        nc.vector.memset(xt_s[:].bitcast(I32), 0)
        for b in range(2):
            for t in range(PACK):
                nc.vector.memset(boards[b][t][:].bitcast(I32), 0)

        load_scales_repeated(w_raw_s, w_scales)
        load_words(xt_w, xt_words[0])
        l1 = load_list(lists, offs, "l1")
        l2 = load_list(lists, offs2, "l2")
        load_words(w_raw, w_words[0].rearrange("p n t -> p (n t)"))
        load_scales(xt_s, xt_scales)
        load_words(w2_raw, w2_words[0].rearrange("p n t -> p (n t)"))
        l3 = load_list(lists, offs3, "l3")
        load_scales_repeated(w2_raw_s, w2_scales)
        l4 = load_list(lists, offs4, "l4")
        l5 = load_list(lists, offs5, "l5")
        l6 = load_list(lists, offs6, "l6")
        for h in range(2):
            nc.sync.dma_start(tz_rows[h][:], tz[P * h : P * (h + 1), :])
        l7 = load_list(lists, offs7, "l7")
        load_words(ws_w, ws_words[0].rearrange("p n t -> p (n t)"))
        load_words(sx_w, sx_words[0].rearrange("p n t -> p (n t)"))
        load_words(wb_w, wb_words[0])
        load_scales(ws_s, ws_scales)
        load_scales(sx_s, sx_scales)
        load_scales(wb_s, wb_scales)

        xg_w = [keep.tile([P, J], U16, align_bytes=64, name=f"xg_w{b}") for b in range(2)]
        xg_s = [keep.tile([P, J], U8, align_bytes=64, name=f"xg_s{b}") for b in range(2)]
        dealt = [keep.tile([P, R], U32, align_bytes=64, name=f"dealt{b}") for b in range(2)]
        dealt_s = [keep.tile([P, R], U8, align_bytes=64, name=f"dealt_s{b}") for b in range(2)]

        def deal_words(b, raw):
            nc.scalar.copy(
                dealt[b][:].rearrange("p (t c i) -> p c t i", t=PACK, i=4),
                raw[:].rearrange("p (c i t) -> p c t i", t=PACK, i=4),
            )

        def deal_scales(b, raw_s):
            nc.vector.tensor_copy(
                dealt_s[b][:].rearrange("p (t m) -> p t m", t=PACK),
                raw_s[:].rearrange("p (m t) -> p t m", t=PACK),
            )

        def first_stage(b, fmt, banks):
            for t in range(PACK):
                cols = slice(P * t, P * (t + 1))
                nc.tensor.matmul_mx(
                    out=banks[t], lhsT=dealt[b][:, cols].bitcast(fmt), lhsT_scale=dealt_s[b][:, cols],
                    rhs=xg_w[b][:].bitcast(E2M1), rhs_scale=xg_s[b][:], start=True, stop=True,
                )

        deal_scales(0, w_raw_s)
        deal_words(0, w_raw)
        deal_words(1, w2_raw)
        for b, tokens in enumerate((l1, l2)):
            nc.vector.tensor_copy(xg_w[b][:], xt_w[:].indirect(tokens[:]))
        for b, tokens in enumerate((l1, l2)):
            nc.vector.tensor_copy(xg_s[b][:], xt_s[:].indirect(tokens[:]))
        a_banks = [psum.tile([P, J], F32, name=f"a{t}") for t in range(PACK)]
        b_banks = [psum.tile([P, 2, J], F32, name=f"b{u}", tag=f"late{u}") for u in range(2)]
        first_stage(0, E4M3, [a_banks[t][:] for t in range(PACK)])
        deal_scales(1, w2_raw_s)
        first_stage(1, E5M2, [b_banks[t % 2][:, t // 2, :] for t in range(PACK)])

        a_sb = [keep.tile([P, J], F32, name=f"a_sb{t}") for t in range(PACK - 1)]
        a_sb.append(keep.tile([P, J], F32, align_bytes=64, name="a_sb3", tag="reused"))
        b_sb = [keep.tile([P, 2, J], F32, name=f"b_sb{u}") for u in range(2)]
        picked = [keep.tile([P, PACK, O], F32, name=f"picked{b}") for b in range(2)]
        put, get = (l3, l4), (l5, l6)

        def scatter(engine, b, t):
            src = a_sb[t][:] if b == 0 else b_sb[t % 2][:, t // 2, :]
            move(engine, boards[b][t][:].indirect(put[b][:]), src)

        def gather(engine, b, t):
            move(engine, picked[b][:, t, :], boards[b][t][:].indirect(get[b][:]))

        owner = ("scalar", "vector")

        def leave_psum(engine, dst, src):
            if engine == "vector":
                nc.vector.tensor_copy(dst, src)
            else:
                nc.scalar.copy(dst, src)

        for t in range(PACK):
            leave_psum(owner[t % 2], a_sb[t][:], a_banks[t][:])
        for t in range(PACK):
            scatter(owner[t % 2], 0, t)
        for u in (1, 0):
            nc.scalar.copy(b_sb[u][:], b_banks[u][:])
        for t in range(PACK):
            scatter(owner[t % 2], 1, t)
        for t in range(PACK):
            for b in range(2):
                gather(owner[t % 2], b, t)

        p_banks = [psum.tile([P, 2, P], F32, name=f"p{u}", tag=f"late{u}") for u in range(2)]
        for u in range(2):
            reads = slice(P * u, P * (u + 1))
            for h in range(2):
                cols = slice(P * h, P * (h + 1))
                nc.tensor.matmul_mx(
                    out=p_banks[u][:, h, :], lhsT=ws_w[:, cols].bitcast(E4M3), lhsT_scale=ws_s[:, cols],
                    rhs=sx_w[:, reads].bitcast(E4M3), rhs_scale=sx_s[:, reads], start=(h == 0), stop=False,
                )

        entries = keep.tile([P, 2, O], F32, tag="board12")
        for h in range(2):
            nc.scalar.activation(entries[:, h, :], tz_rows[h][:].indirect(l7[:]), COPY)

        hid = [keep.tile([P, P, PACK], BF16, align_bytes=64, name=f"hid{u}") for u in range(2)]
        for u in range(2):
            reads = slice(P * u, P * (u + 1))
            nc.vector.tensor_tensor(
                hid[u][:].rearrange("p (c i) t -> p c t i", i=4),
                picked[0][:, :, reads].rearrange("p t (c i) -> p c t i", i=4),
                picked[1][:, :, reads].rearrange("p t (c i) -> p c t i", i=4),
                ALU.max,
            )
        hid_w = [keep.tile([P, P], U32, align_bytes=64, name=f"hid_w{u}") for u in range(2)]
        hid_s = [keep.tile([P, P], U8, align_bytes=64, name=f"hid_s{u}") for u in range(2)]
        for u in range(2):
            nc.vector.quantize_mx(
                out=hid_w[u][:].bitcast(E5M2), scales=hid_s[u][:], in_=hid[u][:].rearrange("p o t -> p (o t)")
            )
            for h in range(2):
                cols = slice(P * h, P * (h + 1))
                nc.tensor.matmul_mx(
                    out=p_banks[u][:, h, :], lhsT=wb_w[:, cols].bitcast(E2M1), lhsT_scale=wb_s[:, cols],
                    rhs=hid_w[u][:].bitcast(E5M2), rhs_scale=hid_s[u][:], start=False, stop=(h == 1),
                )
        for u in range(2):
            reads = slice(P * u, P * (u + 1))
            result = keep.tile([P, 2, P], F32, name=f"result{u}")
            nc.vector.tensor_tensor(result[:], p_banks[u][:], entries[:, :, reads], ALU.add)
            nc.sync.dma_start(out[:, reads].rearrange("(h p) o -> p h o", h=2), result[:])
